import numpy as np
import ml_dtypes


def mxq(x, axis, fmt="e4m3"):
    dtype, down = {"e4m3": (ml_dtypes.float8_e4m3fn, 7), "e5m2": (ml_dtypes.float8_e5m2, 14)}[fmt]
    v = np.moveaxis(np.asarray(x, np.float32).astype(ml_dtypes.bfloat16).astype(np.float64), axis, -1)
    blocks = v.reshape(v.shape[:-1] + (-1, 32))
    amax = np.abs(blocks).max(-1, keepdims=True)
    byte = np.maximum(np.where(amax > 0, np.frexp(amax)[1] - 1 + 127, 0) - down, 1)
    scale = np.exp2(byte - 127.0)
    codes = (blocks / scale).astype(np.float32).astype(dtype).astype(np.float64)
    return np.moveaxis((codes * scale).reshape(v.shape), -1, axis)


WIDE = False


def mx_kscale(k):
    if not WIDE:
        return np.ones(k)
    levels = np.array([10, -10, 5, -5, 0])
    if k % 512:
        return np.exp2(np.random.permutation(np.resize(levels, k // 32))).repeat(32)
    a = np.empty((k // 512, 16))
    for p in range(k // 512):
        a[p, :8] = np.random.permutation(np.resize(levels, 8))
        for g in range(8):
            far = levels[np.abs(levels - a[p, g]) >= 10]
            a[p, g + 8] = far[np.random.randint(len(far))]
    return np.exp2(a.ravel()).repeat(32)


def f64(x):
    return np.asarray(x).astype(np.float64)


def striped(idx):
    return np.tile(np.asarray(idx).reshape(-1, 16).T, (8, 1)).astype(np.uint16)


def unstriped(offs):
    return offs[:16].T.reshape(-1).astype(np.int64)


E2M1 = np.array([0.0, 0.5, 1.0, 1.5, 2.0, 3.0, 4.0, 6.0, -0.0, -0.5, -1.0, -1.5, -2.0, -3.0, -4.0, -6.0])


def pack_weight(w, fmt):
    k, n = w.shape
    w = f64(np.asarray(w, np.float32).astype(ml_dtypes.bfloat16)).reshape(k // 32, 32, n)
    amax = np.abs(w).max(1)
    if fmt == "e4m3":
        byte = np.frexp(amax)[1] - 1 + 127 - 7
    else:
        mant, ex = np.frexp(amax / 6.0)
        byte = np.where(mant > 0.5, ex, ex - 1) + 127
    byte = np.clip(np.where(amax > 0, byte, 1), 1, 254)
    scaled = (w * np.exp2(127.0 - byte)[:, None, :]).reshape(k, n).astype(np.float32)
    by_word = np.ascontiguousarray(scaled.reshape(k // 512, 128, 4, n).transpose(0, 1, 3, 2))
    if fmt == "e4m3":
        words = by_word.astype(ml_dtypes.float8_e4m3fn).view(np.uint8)
    else:
        c = by_word.astype(ml_dtypes.float4_e2m1fn).view(np.uint8) & 0xF
        words = (c[..., 0::2] | (c[..., 1::2] << 4)).reshape(k // 512, 128, 2 * n)
    return np.ascontiguousarray(words), np.ascontiguousarray(byte.astype(np.uint8).reshape(k // 512, 16, n))


def unpack_weight(words, scales, fmt):
    g, _, n = scales.shape
    words = np.ascontiguousarray(words).reshape(g, 128, n, -1)
    if fmt == "e4m3":
        vals = words.view(ml_dtypes.float8_e4m3fn).astype(np.float64)
    else:
        nib = np.empty((g, 128, n, 4), np.uint8)
        nib[..., 0::2] = words & 0xF
        nib[..., 1::2] = words >> 4
        vals = E2M1[nib]
    vals = vals * np.repeat(np.exp2(scales.astype(np.float64) - 127.0), 8, axis=1)[..., None]
    return vals.transpose(0, 1, 3, 2).reshape(g * 512, n)


D, E, T, I, Q = 512, 512, 1024, 256, 512


def setup_inputs():
    n = np.random.standard_normal
    idx = np.random.permutation(T)[:I]
    idx2 = np.random.permutation(T)[:I]
    fd = mx_kscale(D)
    fq = mx_kscale(Q)
    keysp = pack_weight(n((D, T)) / fd[:, None], "e2m1")
    return {
        "query": (n((D, Q)) * 0.5 / np.sqrt(D) * fd[:, None]).astype(np.float32),
        "qs": (np.random.uniform(8.0, 32.0, (Q, 1)) * fq[:, None]).astype(np.float32),
        "grows": (n((Q, E)) / fq[:, None]).astype(np.float32),
        "vals": (n((E, T))).astype(np.float32),
        "keys_words": keysp[0],
        "keys_scales": keysp[1],
        "lift": (n((E, T)) * 0.4).astype(np.float32),
        "sg": (np.random.uniform(0.5, 2.0, (1, I))).astype(np.float32),
        "old": (n((E, T)) * 1.0).astype(np.float32),
        "fade": (np.random.uniform(0.5, 1.0, (1, T))).astype(np.float32),
        "offs": striped(idx),
        "offs2": striped(idx2),
    }


def reference(query, qs, grows, vals, keys_words, keys_scales, lift, sg, old, fade, offs, offs2):
    idx = unstriped(offs)
    idx2 = unstriped(offs2)
    keysu = unpack_weight(keys_words, keys_scales, "e2m1")
    queryq = mxq(f64(query), 0, "e4m3")
    keysidxg = keysu[:, idx]
    a = queryq.T @ keysidxg
    p = np.exp(a - np.max(a, axis=1, keepdims=True))
    w = p * f64(qs) / np.sum(p, axis=1, keepdims=True)
    growsq = mxq(f64(grows), 0, "e4m3")
    wq = mxq(w, 0, "e4m3")
    c0 = growsq.T @ wq
    l1 = np.exp(f64(lift)[:, idx2])
    x1 = f64(vals)[:, idx] * l1
    vp = np.tanh(x1)
    dx1 = c0 * (1.0 - np.square(vp))
    gs = dx1 * f64(sg)
    gf = np.zeros((E, T))
    gf[:, idx] = gs
    y = f64(old) * f64(fade) + gf
    return y

from contextlib import ExitStack

import concourse.mybir as mybir
from concourse.masks import make_identity

F32 = mybir.dt.float32
BF16 = mybir.dt.bfloat16
I32 = mybir.dt.int32
U32 = mybir.dt.uint32
U16 = mybir.dt.uint16
U8 = mybir.dt.uint8
FP8X4 = mybir.dt.float8_e4m3fn_x4
FP4X4 = mybir.dt.float4_e2m1fn_x4
ACT = mybir.ActivationFunctionType
ALU = mybir.AluOpType

D, E, T, SLOTS, Q = 512, 512, 1024, 256, 512
P = 128
PACK = 4
E_TILES = E // P
T_BLOCKS = T // P
HALF = T // 2
QUERY_SPLIT = 84
WINDOWS = 3

FLOPS = 2 * D * Q * SLOTS + 2 * Q * E * SLOTS


def tile_attend_bvlifted_s_kernel(tc, query, qs, grows, vals, keys_words, keys_scales, lift, sg, old, fade, offs, offs2, out):
    nc = tc.nc
    with ExitStack() as ctx:
        held = ctx.enter_context(tc.tile_pool(name="held", bufs=1))
        ring = ctx.enter_context(tc.tile_pool(name="ring", bufs=2))
        psum = ctx.enter_context(tc.psum_pool(name="psum", bufs=1))

        slots = held.tile([P, SLOTS // 16], U16, name="slots")
        nc.sync.dma_start(slots[:], offs)
        key_words = held.tile([P, T], U16, name="key_words")
        nc.sync.dma_start(key_words[:].bitcast(I32), keys_words[0].bitcast(I32))
        key_scales = held.tile([P, T], U8, name="key_scales")
        nc.gpsimd.memset(key_scales[:].bitcast(I32), 0)
        for g in range(4):
            nc.sync.dma_start(key_scales[32 * g : 32 * g + 4, :].bitcast(I32), keys_scales[0, 4 * g : 4 * g + 4, :].bitcast(I32))
        query_raw, grows_raw = [], []
        for source, halves, label in ((query, query_raw, "query_raw"), (grows, grows_raw, "grows_raw")):
            for h in range(2):
                half = held.tile([P, PACK, 256], F32, name=f"{label}{h}")
                nc.sync.dma_start(half[:], source.rearrange("(p j) c -> p j c", j=PACK)[:, :, h * 256 : (h + 1) * 256])
                halves.append(half)
        row_scale = held.tile([P, PACK], F32, name="row_scale")
        nc.sync.dma_start(row_scale[:], qs.rearrange("(p r) o -> p (r o)", r=PACK))
        lift_slots = held.tile([P, SLOTS // 16], U16, name="lift_slots")
        nc.sync.dma_start(lift_slots[:], offs2)
        vectors = held.tile([P, P], F32, name="vectors")
        nc.vector.memset(vectors[:], 0.0)
        lift_t, vals_t, old_t = [], [], []
        for step in range(E_TILES + 2):
            for source, tiles, label, lag in ((lift, lift_t, "lift", 0), (vals, vals_t, "vals", 1), (old, old_t, "old", 2)):
                m = step - lag
                if 0 <= m < E_TILES:
                    rows = held.tile([P, T], F32, name=f"{label}{m}")
                    nc.sync.dma_start(rows[:], source[m * P : (m + 1) * P, :])
                    tiles.append(rows)
            if step == 0:
                nc.sync.dma_start(vectors[0:T_BLOCKS, :], fade.rearrange("o (c p) -> (o c) p", p=P))
                nc.sync.dma_start(vectors[T_BLOCKS : T_BLOCKS + 2, :], sg.rearrange("o (c p) -> (o c) p", p=P))

        identity = held.tile([P, P], F32, name="identity")
        make_identity(nc, identity[:])
        windows = []
        for m in range(WINDOWS):
            window = held.tile([P, T], F32, name=f"window{m}")
            (nc.vector if m == 0 else nc.gpsimd).memset(window[:], 0.0)
            windows.append(window)

        slot_words = held.tile([P, SLOTS], U16, name="slot_words", align_bytes=64)
        slot_scales = held.tile([P, SLOTS], U8, name="slot_scales", align_bytes=64)
        nc.vector.tensor_copy(slot_words[:], key_words[:].indirect(slots[:]))
        nc.vector.tensor_copy(slot_scales[:], key_scales[:].indirect(slots[:]))

        query_bf = held.tile([P, PACK, P, PACK], BF16, name="query_bf", align_bytes=64)
        q_dst = query_bf[:].rearrange("p r s j -> p s j r")
        q_src = [half[:].rearrange("p j (s r) -> p s j r", r=PACK) for half in query_raw]
        nc.scalar.activation(q_dst[:, :64], q_src[0], ACT.Copy)
        nc.vector.tensor_copy(q_dst[:, 64:], q_src[1])
        query_codes = held.tile([P, Q], U32, name="query_codes", align_bytes=64)
        query_scales = held.tile([P, Q], U8, name="query_scales", align_bytes=64)
        banks = []
        for b in range(2):
            cols = slice(2 * b * P, 2 * (b + 1) * P)
            nc.vector.quantize_mx(
                out=query_codes[:, cols].bitcast(FP8X4),
                scales=query_scales[:, cols],
                in_=query_bf[:, 2 * b : 2 * b + 2].rearrange("p r s j -> p (r s j)"),
            )
            bank = psum.tile([P, 2, SLOTS], F32, name="scores", tag="product", bufs=2)
            for h in range(2):
                rcols = slice((2 * b + h) * P, (2 * b + h + 1) * P)
                nc.tensor.matmul_mx(
                    out=bank[:, h, :],
                    lhsT=query_codes[:, rcols].bitcast(FP8X4),
                    lhsT_scale=query_scales[:, rcols],
                    rhs=slot_words[:].bitcast(FP4X4),
                    rhs_scale=slot_scales[:],
                    start=True,
                    stop=True,
                )
            banks.append(bank)

        neg_max = held.tile([P, PACK], F32, name="neg_max")
        sums = held.tile([P, PACK], F32, name="sums")
        inverse = held.tile([P, PACK], F32, name="inverse")
        probs = held.tile([P, PACK, SLOTS], F32, name="probs", tag="probs", align_bytes=64)
        weights_bf = held.tile([P, SLOTS, PACK], BF16, name="weights_bf", align_bytes=64)
        for b in range(2):
            nc.vector.tensor_reduce(neg_max[:, 2 * b : 2 * b + 2], banks[b][:], mybir.AxisListType.X, ALU.max, negate=True)
        for r in range(PACK):
            nc.scalar.activation(probs[:, r, :], banks[r // 2][:, r % 2, :], ACT.Exp, bias=neg_max[:, r : r + 1], accum_out=sums[:, r : r + 1])
            nc.vector.reciprocal(inverse[:, r : r + 1], sums[:, r : r + 1])
            nc.vector.tensor_scalar(weights_bf[:, :, r], probs[:, r, :], inverse[:, r : r + 1], row_scale[:, r : r + 1], ALU.mult, ALU.mult)
        weight_codes = held.tile([P, SLOTS], U32, name="weight_codes", align_bytes=64)
        weight_scales = held.tile([P, SLOTS], U8, name="weight_scales", align_bytes=64)
        nc.vector.quantize_mx(out=weight_codes[:].bitcast(FP8X4), scales=weight_scales[:], in_=weights_bf[:].rearrange("p i r -> p (i r)"))

        turned = psum.tile([P, PACK, P], F32, name="turned", tag="turn", bufs=3)
        nc.tensor.transpose(turned[:, 0, :], vectors[:], identity[:])
        columns = held.tile([P, 16], F32, name="columns")
        nc.scalar.activation(columns[:], turned[:, 0, 0:16], ACT.Copy)
        spread = psum.tile([P, PACK, P], F32, name="spread", tag="turn", bufs=3)
        for c in range(2):
            nc.tensor.transpose(spread[:, c, :], columns[:, T_BLOCKS + c : T_BLOCKS + c + 1].to_broadcast([P, P]), identity[:])
        gain = held.tile([P, SLOTS], F32, name="gain")
        nc.scalar.activation(gain[:], spread[:, 0:2, :].rearrange("p c n -> p (c n)"), ACT.Copy)

        grows_codes = held.tile([P, E], U32, name="grows_codes", align_bytes=64)
        grows_scales = held.tile([P, E], U8, name="grows_scales", align_bytes=64)
        c0_banks = []
        for b in range(2):
            cols = slice(2 * b * P, 2 * (b + 1) * P)
            grows_bf = held.tile([P, 256, PACK], BF16, name="grows_bf", tag=("grows_bf", "probs")[b], align_bytes=64)
            nc.scalar.copy(grows_bf[:].rearrange("p (c i) j -> p c j i", i=PACK), grows_raw[b][:].rearrange("p j (c i) -> p c j i", i=PACK))
            nc.vector.quantize_mx(
                out=grows_codes[:, cols].bitcast(FP8X4),
                scales=grows_scales[:, cols],
                in_=grows_bf[:].rearrange("p e j -> p (e j)"),
            )
            bank = psum.tile([P, 2, SLOTS], F32, name="c0", tag="product", bufs=2)
            for h in range(2):
                ecols = slice((2 * b + h) * P, (2 * b + h + 1) * P)
                nc.tensor.matmul_mx(
                    out=bank[:, h, :],
                    lhsT=grows_codes[:, ecols].bitcast(FP8X4),
                    lhsT_scale=grows_scales[:, ecols],
                    rhs=weight_codes[:].bitcast(FP8X4),
                    rhs_scale=weight_scales[:],
                    start=True,
                    stop=True,
                )
            c0_banks.append(bank)

        lifted, squares = {}, {}

        def lift_factor(m):
            picked = ring.tile([P, SLOTS], F32, name="picked")
            nc.vector.tensor_copy(picked[:], lift_t[m][:].indirect(lift_slots[:]))
            lifted[m] = held.tile([P, SLOTS], F32, name="lifted", tag=f"shared{m}")
            nc.scalar.activation(lifted[m][:], picked[:], ACT.Exp)

        def prepare(m):
            x1 = ring.tile([P, SLOTS], F32, name="x1")
            nc.vector.tensor_tensor(x1[:], vals_t[m][:].indirect(slots[:]), lifted[m][:], ALU.mult)
            vp = ring.tile([P, SLOTS], F32, name="vp")
            nc.scalar.activation(vp[:], x1[:], ACT.Tanh)
            squares[m] = ring.tile([P, SLOTS], F32, name="square")
            nc.scalar.activation(squares[m][:], vp[:], ACT.Square)

        def scatter(m):
            slope = held.tile([P, SLOTS], F32, name="slope", tag=f"shared{m + 1}")
            nc.vector.scalar_tensor_tensor(slope[:], squares[m][:], 1.0, gain[:], ALU.subtract, ALU.mult)
            neg_c0 = ring.tile([P, SLOTS], F32, name="neg_c0")
            nc.scalar.activation(neg_c0[:], c0_banks[m // 2][:, m % 2, :], ACT.Copy, scale=-1.0)
            nc.vector.tensor_tensor(windows[m % WINDOWS][:].indirect(slots[:]), neg_c0[:], slope[:], ALU.mult)

        def finish(m):
            result = held.tile([P, T], F32, name=f"result{m}")
            for h in range(2):
                old_turned = psum.tile([P, PACK, P], F32, name="old_turned", tag="turn", bufs=3)
                for c in range(PACK):
                    t0 = h * HALF + c * P
                    nc.tensor.transpose(old_turned[:, c, :], old_t[m][:, t0 : t0 + P], identity[:])
                faded_turned = ring.tile([P, PACK, P], F32, name="faded_turned", bufs=4)
                for c in range(PACK):
                    k = h * PACK + c
                    nc.scalar.activation(faded_turned[:, c, :], old_turned[:, c, :], ACT.Copy, scale=columns[:, k : k + 1])
                faded = psum.tile([P, PACK, P], F32, name="faded", tag="back", bufs=3)
                for c in range(PACK):
                    nc.tensor.transpose(faded[:, c, :], faded_turned[:, c, :], identity[:])
                tcols = slice(h * HALF, (h + 1) * HALF)
                nc.vector.tensor_tensor(result[:, tcols], faded[:].rearrange("p c n -> p (c n)"), windows[m % WINDOWS][:, tcols], ALU.add)
                if m == E_TILES - 1:
                    nc.sync.dma_start(out[m * P : (m + 1) * P, tcols], result[:, tcols])
            if m < E_TILES - 1:
                nc.sync.dma_start(out[m * P : (m + 1) * P, :], result[:])

        for step in range(E_TILES + 2):
            for stage, lag in ((lift_factor, 0), (prepare, 1), (scatter, 2), (finish, 2)):
                if 0 <= step - lag < E_TILES:
                    stage(step - lag)
